import numpy as np
import ml_dtypes


def mxq(x, axis, fmt="e4m3"):
    dtype, down = {"e4m3": (ml_dtypes.float8_e4m3fn, 7), "e5m2": (ml_dtypes.float8_e5m2, 14)}[fmt]
    v = np.moveaxis(np.asarray(x, np.float32).astype(ml_dtypes.bfloat16).astype(np.float64), axis, -1)
    blocks = v.reshape(v.shape[:-1] + (-1, 32))
    amax = np.abs(blocks).max(-1, keepdims=True)
    byte = np.maximum(np.where(amax > 0, np.frexp(amax)[1] - 1 + 127, 0) - down, 1)
    scale = np.exp2(byte - 127.0)
    codes = (blocks / scale).astype(np.float32).astype(dtype).astype(np.float64)
    return np.moveaxis((codes * scale).reshape(v.shape), -1, axis)


WIDE = False


def mx_kscale(k):
    if not WIDE:
        return np.ones(k)
    levels = np.array([10, -10, 5, -5, 0])
    if k % 512:
        return np.exp2(np.random.permutation(np.resize(levels, k // 32))).repeat(32)
    a = np.empty((k // 512, 16))
    for p in range(k // 512):
        a[p, :8] = np.random.permutation(np.resize(levels, 8))
        for g in range(8):
            far = levels[np.abs(levels - a[p, g]) >= 10]
            a[p, g + 8] = far[np.random.randint(len(far))]
    return np.exp2(a.ravel()).repeat(32)


def f64(x):
    return np.asarray(x).astype(np.float64)


def striped(idx):
    return np.tile(idx.reshape(-1, 16).T, (8, 1)).astype(np.uint16)


def unstriped(offs):
    return offs[:16].T.reshape(-1).astype(np.int64)


def striped8(idx):
    return np.concatenate([x.reshape(-1, 16).T for x in idx]).astype(np.uint16)


def runs(offs, k):
    lists = np.stack([offs[16 * r : 16 * r + 16].T.reshape(-1) for r in range(8)]).astype(np.int64)
    return lists[np.arange(k) % 512 // 64]


def pack_weight(w):
    k, n = w.shape
    w = f64(np.asarray(w, np.float32).astype(ml_dtypes.bfloat16)).reshape(k // 32, 32, n)
    amax = np.abs(w).max(1)
    byte = np.clip(np.where(amax > 0, np.frexp(amax)[1] - 1 + 127 - 7, 1), 1, 254)
    scaled = (w * np.exp2(127.0 - byte)[:, None, :]).reshape(k, n).astype(np.float32)
    words = np.ascontiguousarray(scaled.reshape(k // 512, 128, 4, n).transpose(0, 1, 3, 2)).astype(ml_dtypes.float8_e4m3fn).view(np.uint8)
    return words, np.ascontiguousarray(byte.astype(np.uint8).reshape(k // 512, 16, n))


def unpack_weight(words, scales):
    g, p, n, _ = words.shape
    vals = np.ascontiguousarray(words).view(ml_dtypes.float8_e4m3fn).astype(np.float64) * np.repeat(np.exp2(scales.astype(np.float64) - 127.0), 8, axis=1)[..., None]
    return vals.transpose(0, 1, 3, 2).reshape(g * 512, n)


def relu(v):
    return np.maximum(v, 0.0)


K, T, S, H, W = 512, 2048, 512, 512, 256


def setup_inputs():
    n = np.random.standard_normal
    s = mx_kscale(K)[:, None]
    u = mx_kscale(S)
    packed_xT = pack_weight(n((K, T)) * s)
    perm = np.stack([np.random.permutation(S) for _ in range(8)])
    return {
        "x_words": packed_xT[0],
        "x_scales": packed_xT[1],
        "w1": (n((K, H)) / np.sqrt(K) / s).astype(np.float32),
        "ga": (np.random.uniform(0.5, 1.5, (H, 1)) * u[:, None]).astype(np.float32),
        "gb": (np.random.uniform(0.5, 1.5, (H, 1)) / u[:, None]).astype(np.float32),
        "offs": striped(np.random.permutation(T)[:S]),
        "n1": striped8(np.stack([np.random.permutation(S) for _ in range(8)])),
        "n2": striped8(np.stack([np.random.permutation(S) for _ in range(8)])),
        "n3": striped8(perm[:, :W]),
        "n4": striped8(perm[:, W:]),
        "n5": striped8(np.stack([np.random.permutation(S) for _ in range(8)])),
        "n6": striped8(np.stack([np.random.permutation(S) for _ in range(8)])),
    }


def reference(x_words, x_scales, w1, ga, gb, offs, n1, n2, n3, n4, n5, n6):
    xq = unpack_weight(x_words, x_scales)[:, unstriped(offs)]
    y = mxq(f64(w1), 0, "e4m3").T @ xq
    st = y - (y[np.arange(H)[:, None], runs(n1, H)])
    z = f64(ga) * (st / (np.abs(st[np.arange(H)[:, None], runs(n2, H)]) + 0.5))
    pa = y[np.arange(H)[:, None], runs(n3, H)]
    pb = y[np.arange(H)[:, None], runs(n4, H)]
    ra = pa - (0.5 * pb)
    ds = y.copy()
    ds[np.arange(H)[:, None], runs(n4, H)] = ra
    z2 = f64(gb) * (ds - (0.5 * (ds[np.arange(H)[:, None], runs(n5, H)])))
    s = 0.0625 * ((mxq(z, 0, "e4m3").T @ mxq(z2, 0, "e4m3")))
    rl = relu(s)
    ds2 = np.zeros((S, S))
    ds2[np.arange(S)[:, None], runs(n6, S)] = rl
    return ds2 - (0.5 * s)

@@ -1,0 +1,244 @@
+from contextlib import ExitStack
+
+import concourse.mybir as mybir
+from concourse.masks import make_identity
+
+F32 = mybir.dt.float32
+BF16 = mybir.dt.bfloat16
+I32 = mybir.dt.int32
+U32 = mybir.dt.uint32
+U16 = mybir.dt.uint16
+U8 = mybir.dt.uint8
+FP8X4 = mybir.dt.float8_e4m3fn_x4
+ACT = mybir.ActivationFunctionType
+ALU = mybir.AluOpType
+
+P = 128
+PACK = 4
+T = 2048
+S = 512
+HALF = S // 2
+FLOPS = 2 * 2 * 512 * 512 * 512
+
+
+def tile_picked_selfhopnfolddsend_none_p_kernel(tc, x_words, x_scales, w1, ga, gb, offs, n1, n2, n3, n4, n5, n6, out):
+    nc = tc.nc
+    with ExitStack() as ctx:
+        sb = ctx.enter_context(tc.tile_pool(name="sb", bufs=1))
+        psum = ctx.enter_context(tc.psum_pool(name="psum", bufs=1))
+
+        def list_tile(name, src):
+            t = sb.tile([P, src.shape[1]], U16, name=name)
+            nc.sync.dma_start(t[:], src)
+            return t
+
+        xs = sb.tile([P, T], U8, name="xs", tag="xs", align_bytes=64)
+        nc.vector.memset(xs[:].bitcast(I32), 0)
+        one = sb.tile([P, 1], F32, name="one")
+        nc.gpsimd.memset(one[:], 1.0)
+        w_rows = w1.rearrange("(p j) c -> p j c", j=PACK)
+        w_raw = []
+        for h in range(2):
+            wr = sb.tile([P, PACK, HALF], F32, name="w_raw%d" % h)
+            nc.sync.dma_start(wr[:], w_rows[:, :, h * HALF : (h + 1) * HALF])
+            w_raw.append(wr)
+            if h == 0:
+                for q in range(4):
+                    nc.sync.dma_start(xs[32 * q : 32 * q + 4, :].bitcast(I32), x_scales[0, 4 * q : 4 * q + 4, :].bitcast(I32))
+        offs_t = list_tile("offs_t", offs)
+        xw = sb.tile([P, T], U32, name="xw", align_bytes=64)
+        nc.sync.dma_start(xw[:].bitcast(I32), x_words[0].rearrange("p n t -> p (n t)").bitcast(I32))
+        ga_t = sb.tile([P, PACK], F32, name="ga_t")
+        gb_t = sb.tile([P, PACK], F32, name="gb_t")
+        nc.gpsimd.dma_start(ga_t[:], ga.rearrange("(p t) o -> p (t o)", t=PACK))
+        nc.gpsimd.dma_start(gb_t[:], gb.rearrange("(p t) o -> p (t o)", t=PACK))
+        n1_t = list_tile("n1_t", n1)
+        n4_t = list_tile("n4_t", n4)
+        n3_t = list_tile("n3_t", n3)
+        n5_t = list_tile("n5_t", n5)
+        n2_t = list_tile("n2_t", n2)
+        n6_t = list_tile("n6_t", n6)
+
+        warm = sb.tile([P, 1], F32, name="warm")
+        nc.scalar.activation(warm[:], one[:], ACT.Ln)
+        ident = sb.tile([P, P], F32, name="ident")
+        make_identity(nc, ident[:])
+
+        xgs = sb.tile([P, S], U8, name="xgs", align_bytes=64)
+        nc.vector.tensor_copy(xgs[:], xs[:].indirect(offs_t[:]))
+        xgw = sb.tile([P, S], U32, name="xgw", tag="xs", align_bytes=64)
+        nc.vector.tensor_copy(xgw[:], xw[:].indirect(offs_t[:]))
+
+        safe = sb.tile([P, PACK], F32, name="safe")
+        nc.vector.scalar_tensor_tensor(safe[:], ga_t[:], 0.0, ga_t[:], ALU.is_equal, ALU.add)
+        inv = sb.tile([P, PACK], F32, name="inv")
+        nc.vector.reciprocal(inv[:], safe[:])
+
+        w_bf = sb.tile([P, PACK, P, PACK], BF16, name="w_bf", align_bytes=64)
+        M2 = P // 2
+        for h in range(2):
+            nc.scalar.copy(
+                w_bf[:, :, h * M2 : (h + 1) * M2, :].rearrange("p t m j -> p m j t"),
+                w_raw[h][:].rearrange("p j (m t) -> p m j t", t=PACK),
+            )
+        wq = sb.tile([P, S], U32, name="wq", align_bytes=64)
+        wsc = sb.tile([P, S], U8, name="wsc", align_bytes=64)
+        y_ps = []
+        for t in range(PACK):
+            cols = slice(t * P, (t + 1) * P)
+            nc.vector.quantize_mx(out=wq[:, cols].bitcast(FP8X4), scales=wsc[:, cols], in_=w_bf[:, t].rearrange("p m j -> p (m j)"))
+            pieces = []
+            for lo, hi, tag in ((0, HALF, "y0"), (HALF, S, "s0")) if t == 0 else ((0, S, "y%d" % t),):
+                bank = psum.tile([P, S], F32, name="y%d_%d" % (t, lo), tag=tag)
+                nc.tensor.matmul_mx(out=bank[:, lo:hi], lhsT=wq[:, cols].bitcast(FP8X4), lhsT_scale=wsc[:, cols],
+                                    rhs=xgw[:, lo:hi].bitcast(FP8X4), rhs_scale=xgs[:, lo:hi], start=True, stop=True)
+                pieces.append((slice(lo, hi), bank))
+            y_ps.append(pieces)
+
+        def scaled_y(dst, t, gain):
+            for cols, bank in y_ps[t]:
+                nc.scalar.activation(dst[:, cols], bank[:, cols], ACT.Copy, scale=gain[:, t : t + 1])
+
+        ds = [sb.tile([P, S + HALF], F32, name="ds%d" % t) for t in range(PACK)]
+        pb0 = sb.tile([P, HALF], F32, name="pb0")
+        pb = [pb0[:]] + [ds[t][:, S:] for t in range(PACK - 1)]
+        pa = [sb.tile([P, HALF], F32, name="pa%d" % t) for t in range(PACK)]
+
+        def fetch_pairs(t):
+            nc.vector.tensor_scalar(pb[t], ds[t][:].indirect(n4_t[:]), -0.5, 0.0, ALU.mult, ALU.add)
+            nc.vector.tensor_copy(pa[t][:], ds[t][:].indirect(n3_t[:]))
+
+        def put_pairs(t):
+            nc.vector.tensor_tensor(ds[t][:].indirect(n4_t[:]), pa[t][:], pb[t], ALU.add)
+
+        (cols_a, bank_a), (cols_b, bank_b) = y_ps[0]
+        nc.scalar.activation(ds[0][:, cols_a], bank_a[:, cols_a], ACT.Copy, scale=gb_t[:, 0:1])
+        nc.vector.tensor_scalar(ds[0][:, cols_b], bank_b[:, cols_b], gb_t[:, 0:1], None, ALU.mult)
+        fetch_pairs(0)
+
+        gst = sb.tile([P, PACK, S], F32, name="gst")
+        for t in range(PACK):
+            ya = sb.tile([P, 2 * S], F32, name="ya%d" % t)
+            ya2 = sb.tile([P, S], F32, name="ya2%d" % t)
+            scaled_y(ya, t, ga_t)
+            scaled_y(ya2, t, ga_t)
+            nc.vector.tensor_tensor(gst[:, t, :], ya[:].indirect(n1_t[:]), ya2[:], ALU.subtract)
+
+        for t in range(1, PACK):
+            scaled_y(ds[t], t, gb_t)
+            fetch_pairs(t)
+            put_pairs(t - 1)
+        put_pairs(PACK - 1)
+
+        logs = []
+        for t in range(PACK):
+            lg = sb.tile([P, 2 * S], F32, name="lg%d" % t)
+            nc.scalar.activation(lg[:, S:], gst[:, t, :], ACT.Abs, scale=inv[:, t : t + 1])
+            logs.append(lg)
+        for t in range(PACK):
+            nc.scalar.activation(logs[t][:, :S], logs[t][:, S:], ACT.Ln, bias=0.5)
+
+        rg = sb.tile([P, PACK, S], F32, name="rg")
+        z2 = sb.tile([P, PACK, S], F32, name="z2")
+        half_ds = []
+
+        def halve(t):
+            hd = sb.tile([P, S], F32, name="hd%d" % t)
+            nc.scalar.activation(hd[:], ds[t][:, :S], ACT.Copy, scale=0.5)
+            half_ds.append(hd)
+
+        def recip(t):
+            nc.scalar.activation(rg[:, t, :], logs[t][:].indirect(n2_t[:]), ACT.Exp, scale=-1.0)
+
+        halve(0)
+        halve(1)
+        recip(0)
+        halve(2)
+        recip(1)
+        halve(3)
+        recip(2)
+        recip(3)
+        for h in range(2):
+            cols = slice(h * HALF, (h + 1) * HALF)
+            for t in range(PACK):
+                nc.vector.tensor_tensor(z2[:, t, cols], half_ds[t][:].indirect(n5_t[:, h * 16 : (h + 1) * 16]), ds[t][:, cols], ALU.subtract)
+
+        zq = sb.tile([P, S], U32, name="zq", align_bytes=64)
+        zs = sb.tile([P, S], U8, name="zs", align_bytes=64)
+        z2q = sb.tile([P, S], U32, name="z2q", align_bytes=64)
+        z2s = sb.tile([P, S], U8, name="z2s", align_bytes=64)
+
+        def product(h):
+            us = slice(2 * h, 2 * h + 2)
+            z_bf = sb.tile([P, 2, P, PACK], BF16, name="z_bf%d" % h, tag="bf%d" % h, align_bytes=64)
+            nc.vector.tensor_tensor(
+                z_bf[:].rearrange("p u m t -> p m t u"),
+                gst[:].rearrange("p t (m u) -> p m t u", u=PACK)[:, :, :, us],
+                rg[:].rearrange("p t (m u) -> p m t u", u=PACK)[:, :, :, us],
+                ALU.mult,
+            )
+            cols = slice(h * HALF, (h + 1) * HALF)
+            nc.vector.quantize_mx(out=zq[:, cols].bitcast(FP8X4), scales=zs[:, cols], in_=z_bf[:].rearrange("p u m t -> p (u m t)"))
+
+        def weave(h):
+            cols = slice(h * HALF, (h + 1) * HALF)
+            z2_bf = sb.tile([P, HALF, PACK], BF16, name="z2_bf%d" % h, tag="bf%d" % (1 + h), align_bytes=64)
+            nc.scalar.copy(
+                z2_bf[:].rearrange("p (c i) t -> p c t i", i=4),
+                z2[:, :, cols].rearrange("p t (c i) -> p c t i", i=4),
+            )
+            nc.vector.quantize_mx(out=z2q[:, cols].bitcast(FP8X4), scales=z2s[:, cols], in_=z2_bf[:].rearrange("p j t -> p (j t)"))
+
+        product(0)
+        weave(0)
+        product(1)
+        weave(1)
+
+        s_ps = [psum.tile([P, S], F32, name="s%d" % u, tag="s%d" % u) for u in range(PACK)]
+        rl = [sb.tile([P, S], F32, name="rl%d" % u) for u in range(PACK)]
+        hs = [sb.tile([P, S], F32, name="hs%d" % u) for u in range(PACK - 1)]
+        ds2 = [sb.tile([P, S if u < 2 else 2 * S], F32, name="ds2%d" % u) for u in range(PACK)]
+        out_rows = out.rearrange("(m u) j -> u m j", u=PACK)
+
+        def send(u, lo, hi):
+            cols = slice(lo, hi)
+            rows = slice(u * P, (u + 1) * P)
+            bank = s_ps[u] if hi == S else psum.tile([P, S], F32, name="early%d" % u, tag="y%d" % (2 + u))
+            nc.tensor.matmul_mx(out=bank[:, cols], lhsT=zq[:, rows].bitcast(FP8X4), lhsT_scale=zs[:, rows],
+                                rhs=z2q[:, cols].bitcast(FP8X4), rhs_scale=z2s[:, cols], start=True, stop=True)
+            nc.scalar.activation(rl[u][:, cols], bank[:, cols], ACT.Relu, scale=0.0625)
+            nc.vector.tensor_copy(ds2[u][:].indirect(n6_t[:, lo // 16 : hi // 16]), rl[u][:, cols])
+            if u < PACK - 1:
+                nc.scalar.activation(hs[u][:, cols], bank[:, cols], ACT.Copy, scale=-0.03125)
+
+        def finish(u):
+            res = sb.tile([P, S], F32, name="res%d" % u)
+            if u == PACK - 1:
+                for h in range(2):
+                    cols = slice(h * HALF, (h + 1) * HALF)
+                    nc.vector.scalar_tensor_tensor(res[:, cols], s_ps[u][:, cols], -0.03125, ds2[u][:, cols], ALU.mult, ALU.add)
+                    nc.sync.dma_start(out_rows[u][:, cols], res[:, cols])
+            else:
+                turned = psum.tile([P, S], F32, name="turned%d" % u, tag="y%d" % (u % 2))
+                for k, term in enumerate((hs[u], ds2[u])):
+                    for b in range(PACK):
+                        blk = slice(b * P, (b + 1) * P)
+                        nc.tensor.matmul(turned[:, blk], term[:, blk], ident[:], is_transpose=True,
+                                         start=(k == 0 and b == 0), stop=(k == 1 and b == PACK - 1))
+                turned_sb = sb.tile([P, S], F32, name="turned_sb%d" % u)
+                nc.scalar.copy(turned_sb[:], turned[:])
+                back = psum.tile([P, S], F32, name="back%d" % u, tag="y%d" % (2 + u % 2))
+                for b in range(PACK):
+                    blk = slice(b * P, (b + 1) * P)
+                    nc.tensor.transpose(back[:, blk], turned_sb[:, blk], ident[:])
+                nc.scalar.copy(res[:], back[:])
+                nc.scalar.dma_start(out_rows[u], res[:])
+
+        send(0, 0, HALF)
+        send(1, 0, HALF)
+        send(0, HALF, S)
+        send(1, HALF, S)
+        send(2, 0, S)
+        send(3, 0, S)
+        for u in range(PACK):
+            finish(u)

@@ -34,35 +34,33 @@ def tile_picked_selfhopnfolddsend_none_p_kernel(tc, x_words, x_scales, w1, ga, g
 
         xs = sb.tile([P, T], U8, name="xs", tag="xs", align_bytes=64)
         nc.vector.memset(xs[:].bitcast(I32), 0)
-        one = sb.tile([P, 1], F32, name="one")
-        nc.gpsimd.memset(one[:], 1.0)
         w_rows = w1.rearrange("(p j) c -> p j c", j=PACK)
-        w_raw = []
-        for h in range(2):
-            wr = sb.tile([P, PACK, HALF], F32, name="w_raw%d" % h)
-            nc.sync.dma_start(wr[:], w_rows[:, :, h * HALF : (h + 1) * HALF])
-            w_raw.append(wr)
-            if h == 0:
-                for q in range(4):
-                    nc.sync.dma_start(xs[32 * q : 32 * q + 4, :].bitcast(I32), x_scales[0, 4 * q : 4 * q + 4, :].bitcast(I32))
+        w_raw = [sb.tile([P, PACK, HALF], F32, name="w_raw%d" % h) for h in range(2)]
+        nc.sync.dma_start(w_raw[0][:], w_rows[:, :, :HALF])
+        for q in range(4):
+            nc.sync.dma_start(xs[32 * q : 32 * q + 4, :].bitcast(I32), x_scales[0, 4 * q : 4 * q + 4, :].bitcast(I32))
         offs_t = list_tile("offs_t", offs)
         xw = sb.tile([P, T], U32, name="xw", align_bytes=64)
         nc.sync.dma_start(xw[:].bitcast(I32), x_words[0].rearrange("p n t -> p (n t)").bitcast(I32))
+        nc.sync.dma_start(w_raw[1][:], w_rows[:, :, HALF:])
         ga_t = sb.tile([P, PACK], F32, name="ga_t")
         gb_t = sb.tile([P, PACK], F32, name="gb_t")
-        nc.gpsimd.dma_start(ga_t[:], ga.rearrange("(p t) o -> p (t o)", t=PACK))
-        nc.gpsimd.dma_start(gb_t[:], gb.rearrange("(p t) o -> p (t o)", t=PACK))
-        n1_t = list_tile("n1_t", n1)
+        nc.sync.dma_start(gb_t[:], gb.rearrange("(p t) o -> p (t o)", t=PACK))
+        nc.sync.dma_start(ga_t[:], ga.rearrange("(p t) o -> p (t o)", t=PACK))
         n4_t = list_tile("n4_t", n4)
         n3_t = list_tile("n3_t", n3)
+        n1_t = list_tile("n1_t", n1)
         n5_t = list_tile("n5_t", n5)
         n2_t = list_tile("n2_t", n2)
         n6_t = list_tile("n6_t", n6)
 
+        one = sb.tile([P, 1], F32, name="one")
+        nc.vector.memset(one[:], 1.0)
         warm = sb.tile([P, 1], F32, name="warm")
         nc.scalar.activation(warm[:], one[:], ACT.Ln)
         ident = sb.tile([P, P], F32, name="ident")
-        make_identity(nc, ident[:])
+        nc.vector.memset(ident[:], 0.0)
+        make_identity(nc, ident[:], nomemset=True)
 
         xgs = sb.tile([P, S], U8, name="xgs", align_bytes=64)
         nc.vector.tensor_copy(xgs[:], xs[:].indirect(offs_t[:]))
@@ -77,10 +75,11 @@ def tile_picked_selfhopnfolddsend_none_p_kernel(tc, x_words, x_scales, w1, ga, g
         w_bf = sb.tile([P, PACK, P, PACK], BF16, name="w_bf", align_bytes=64)
         M2 = P // 2
         for h in range(2):
-            nc.scalar.copy(
-                w_bf[:, :, h * M2 : (h + 1) * M2, :].rearrange("p t m j -> p m j t"),
-                w_raw[h][:].rearrange("p j (m t) -> p m j t", t=PACK),
-            )
+            for copy, lo, hi in ((nc.vector.tensor_copy, 0, 40), (nc.scalar.copy, 40, M2)):
+                copy(
+                    w_bf[:, :, h * M2 + lo : h * M2 + hi, :].rearrange("p t m j -> p m j t"),
+                    w_raw[h][:].rearrange("p j (m t) -> p m j t", t=PACK)[:, lo:hi],
+                )
         wq = sb.tile([P, S], U32, name="wq", align_bytes=64)
         wsc = sb.tile([P, S], U8, name="wsc", align_bytes=64)
         y_ps = []
@@ -99,17 +98,16 @@ def tile_picked_selfhopnfolddsend_none_p_kernel(tc, x_words, x_scales, w1, ga, g
             for cols, bank in y_ps[t]:
                 nc.scalar.activation(dst[:, cols], bank[:, cols], ACT.Copy, scale=gain[:, t : t + 1])
 
-        ds = [sb.tile([P, S + HALF], F32, name="ds%d" % t) for t in range(PACK)]
-        pb0 = sb.tile([P, HALF], F32, name="pb0")
-        pb = [pb0[:]] + [ds[t][:, S:] for t in range(PACK - 1)]
-        pa = [sb.tile([P, HALF], F32, name="pa%d" % t) for t in range(PACK)]
+        ds = [sb.tile([P, S + spare * HALF], F32, name="ds%d" % t) for t, spare in enumerate((2, 1, 0, 0))]
+        pa = [sb.tile([P, HALF], F32, name="pa%d" % t)[:] for t in range(3)] + [ds[1][:, S:]]
+        pb = [sb.tile([P, HALF], F32, name="pb%d" % t)[:] for t in range(2)] + [ds[0][:, S : S + HALF], ds[0][:, S + HALF :]]
 
         def fetch_pairs(t):
             nc.vector.tensor_scalar(pb[t], ds[t][:].indirect(n4_t[:]), -0.5, 0.0, ALU.mult, ALU.add)
-            nc.vector.tensor_copy(pa[t][:], ds[t][:].indirect(n3_t[:]))
+            nc.vector.tensor_copy(pa[t], ds[t][:].indirect(n3_t[:]))
 
         def put_pairs(t):
-            nc.vector.tensor_tensor(ds[t][:].indirect(n4_t[:]), pa[t][:], pb[t], ALU.add)
+            nc.vector.tensor_tensor(ds[t][:].indirect(n4_t[:]), pa[t], pb[t], ALU.add)
 
         (cols_a, bank_a), (cols_b, bank_b) = y_ps[0]
         nc.scalar.activation(ds[0][:, cols_a], bank_a[:, cols_a], ACT.Copy, scale=gb_t[:, 0:1])
@@ -127,8 +125,8 @@ def tile_picked_selfhopnfolddsend_none_p_kernel(tc, x_words, x_scales, w1, ga, g
         for t in range(1, PACK):
             scaled_y(ds[t], t, gb_t)
             fetch_pairs(t)
-            put_pairs(t - 1)
-        put_pairs(PACK - 1)
+        for t in range(PACK):
+            put_pairs(t)
 
         logs = []
         for t in range(PACK):
@@ -143,25 +141,24 @@ def tile_picked_selfhopnfolddsend_none_p_kernel(tc, x_words, x_scales, w1, ga, g
         half_ds = []
 
         def halve(t):
-            hd = sb.tile([P, S], F32, name="hd%d" % t)
-            nc.scalar.activation(hd[:], ds[t][:, :S], ACT.Copy, scale=0.5)
+            hd = sb.tile([P, 2 * S], F32, name="hd%d" % t)
+            nc.scalar.activation(hd[:, :S], ds[t][:, :S], ACT.Copy, scale=0.5)
             half_ds.append(hd)
 
         def recip(t):
             nc.scalar.activation(rg[:, t, :], logs[t][:].indirect(n2_t[:]), ACT.Exp, scale=-1.0)
 
+        recip(0)
         halve(0)
         halve(1)
-        recip(0)
-        halve(2)
         recip(1)
+        halve(2)
         halve(3)
         recip(2)
         recip(3)
-        for h in range(2):
-            cols = slice(h * HALF, (h + 1) * HALF)
-            for t in range(PACK):
-                nc.vector.tensor_tensor(z2[:, t, cols], half_ds[t][:].indirect(n5_t[:, h * 16 : (h + 1) * 16]), ds[t][:, cols], ALU.subtract)
+        for t in range(PACK):
+            for lo, hi in ((0, S),) if t < PACK - 1 else ((0, HALF), (HALF, S)):
+                nc.vector.tensor_tensor(z2[:, t, lo:hi], half_ds[t][:].indirect(n5_t[:, lo // 16 : hi // 16]), ds[t][:, lo:hi], ALU.subtract)
 
         zq = sb.tile([P, S], U32, name="zq", align_bytes=64)
         zs = sb.tile([P, S], U8, name="zs", align_bytes=64)
@@ -170,42 +167,49 @@ def tile_picked_selfhopnfolddsend_none_p_kernel(tc, x_words, x_scales, w1, ga, g
 
         def product(h):
             us = slice(2 * h, 2 * h + 2)
-            z_bf = sb.tile([P, 2, P, PACK], BF16, name="z_bf%d" % h, tag="bf%d" % h, align_bytes=64)
+            z_bf = sb.tile([P, 2, P, PACK], BF16, name="z_bf%d" % h, align_bytes=64)
             nc.vector.tensor_tensor(
                 z_bf[:].rearrange("p u m t -> p m t u"),
                 gst[:].rearrange("p t (m u) -> p m t u", u=PACK)[:, :, :, us],
                 rg[:].rearrange("p t (m u) -> p m t u", u=PACK)[:, :, :, us],
                 ALU.mult,
             )
+            return z_bf
+
+        def quantise_z(h, z_bf):
             cols = slice(h * HALF, (h + 1) * HALF)
             nc.vector.quantize_mx(out=zq[:, cols].bitcast(FP8X4), scales=zs[:, cols], in_=z_bf[:].rearrange("p u m t -> p (u m t)"))
 
-        def weave(h):
-            cols = slice(h * HALF, (h + 1) * HALF)
-            z2_bf = sb.tile([P, HALF, PACK], BF16, name="z2_bf%d" % h, tag="bf%d" % (1 + h), align_bytes=64)
+        def weave(lo, hi):
+            z2_bf = sb.tile([P, hi - lo, PACK], BF16, name="z2_bf%d" % lo, align_bytes=64)
             nc.scalar.copy(
                 z2_bf[:].rearrange("p (c i) t -> p c t i", i=4),
-                z2[:, :, cols].rearrange("p t (c i) -> p c t i", i=4),
+                z2[:, :, lo:hi].rearrange("p t (c i) -> p c t i", i=4),
             )
-            nc.vector.quantize_mx(out=z2q[:, cols].bitcast(FP8X4), scales=z2s[:, cols], in_=z2_bf[:].rearrange("p j t -> p (j t)"))
+            nc.vector.quantize_mx(out=z2q[:, lo:hi].bitcast(FP8X4), scales=z2s[:, lo:hi], in_=z2_bf[:].rearrange("p j t -> p (j t)"))
 
-        product(0)
-        weave(0)
-        product(1)
-        weave(1)
+        first = product(0)
+        weave(0, P)
+        quantise_z(0, first)
+        second = product(1)
+        weave(P, HALF)
+        weave(HALF, S)
+        quantise_z(1, second)
 
         s_ps = [psum.tile([P, S], F32, name="s%d" % u, tag="s%d" % u) for u in range(PACK)]
         rl = [sb.tile([P, S], F32, name="rl%d" % u) for u in range(PACK)]
         hs = [sb.tile([P, S], F32, name="hs%d" % u) for u in range(PACK - 1)]
-        ds2 = [sb.tile([P, S if u < 2 else 2 * S], F32, name="ds2%d" % u) for u in range(PACK)]
+        ds2 = [sb.tile([P, 2 * S], F32, name="ds2%d" % u) for u in range(PACK)]
         out_rows = out.rearrange("(m u) j -> u m j", u=PACK)
 
-        def send(u, lo, hi):
+        def send(u, *edges):
+            lo, hi = edges[0], edges[-1]
             cols = slice(lo, hi)
             rows = slice(u * P, (u + 1) * P)
             bank = s_ps[u] if hi == S else psum.tile([P, S], F32, name="early%d" % u, tag="y%d" % (2 + u))
-            nc.tensor.matmul_mx(out=bank[:, cols], lhsT=zq[:, rows].bitcast(FP8X4), lhsT_scale=zs[:, rows],
-                                rhs=z2q[:, cols].bitcast(FP8X4), rhs_scale=z2s[:, cols], start=True, stop=True)
+            for a, b in zip(edges, edges[1:]):
+                nc.tensor.matmul_mx(out=bank[:, a:b], lhsT=zq[:, rows].bitcast(FP8X4), lhsT_scale=zs[:, rows],
+                                    rhs=z2q[:, a:b].bitcast(FP8X4), rhs_scale=z2s[:, a:b], start=True, stop=True)
             nc.scalar.activation(rl[u][:, cols], bank[:, cols], ACT.Relu, scale=0.0625)
             nc.vector.tensor_copy(ds2[u][:].indirect(n6_t[:, lo // 16 : hi // 16]), rl[u][:, cols])
             if u < PACK - 1:
@@ -234,10 +238,10 @@ def tile_picked_selfhopnfolddsend_none_p_kernel(tc, x_words, x_scales, w1, ga, g
                 nc.scalar.copy(res[:], back[:])
                 nc.scalar.dma_start(out_rows[u], res[:])
 
-        send(0, 0, HALF)
-        send(1, 0, HALF)
-        send(0, HALF, S)
-        send(1, HALF, S)
+        send(0, 0, P)
+        send(1, 0, P)
+        send(0, P, HALF, S)
+        send(1, P, HALF, S)
         send(2, 0, S)
         send(3, 0, S)
         for u in range(PACK):

@@ -15,10 +15,16 @@ ALU = mybir.AluOpType
 
 P = 128
 PACK = 4
+QUADRANTS = 4
+STRIPE = 16
+LINE = 4
 T = 2048
 S = 512
 HALF = S // 2
-FLOPS = 2 * 2 * 512 * 512 * 512
+WIDE = 2 * S
+W_PIECES = ((0, 64, 40), (64, 32, 0), (96, 32, 20))
+LAST_STORE = 128
+FLOPS = 2 * 2 * S * S * S
 
 
 def tile_picked_selfhopnfolddsend_none_p_kernel(tc, x_words, x_scales, w1, ga, gb, offs, n1, n2, n3, n4, n5, n6, out):
@@ -27,32 +33,41 @@ def tile_picked_selfhopnfolddsend_none_p_kernel(tc, x_words, x_scales, w1, ga, g
         sb = ctx.enter_context(tc.tile_pool(name="sb", bufs=1))
         psum = ctx.enter_context(tc.psum_pool(name="psum", bufs=1))
 
-        def list_tile(name, src):
-            t = sb.tile([P, src.shape[1]], U16, name=name)
-            nc.sync.dma_start(t[:], src)
-            return t
+        def load_list(name, src):
+            tile = sb.tile([P, src.shape[1]], U16, name=name)
+            nc.sync.dma_start(tile[:], src)
+            return tile
 
-        xs = sb.tile([P, T], U8, name="xs", tag="xs", align_bytes=64)
-        nc.vector.memset(xs[:].bitcast(I32), 0)
+        def entries(list_tile, lo, hi):
+            return list_tile[:, lo // STRIPE : hi // STRIPE]
+
+        x_scale_rows = sb.tile([P, T], U8, name="x_scale_rows", tag="x_scale_rows", align_bytes=64)
+        nc.vector.memset(x_scale_rows[:].bitcast(I32), 0)
         w_rows = w1.rearrange("(p j) c -> p j c", j=PACK)
-        w_raw = [sb.tile([P, PACK, HALF], F32, name="w_raw%d" % h) for h in range(2)]
-        nc.sync.dma_start(w_raw[0][:], w_rows[:, :, :HALF])
-        for q in range(4):
-            nc.sync.dma_start(xs[32 * q : 32 * q + 4, :].bitcast(I32), x_scales[0, 4 * q : 4 * q + 4, :].bitcast(I32))
-        offs_t = list_tile("offs_t", offs)
-        xw = sb.tile([P, T], U32, name="xw", align_bytes=64)
-        nc.sync.dma_start(xw[:].bitcast(I32), x_words[0].rearrange("p n t -> p (n t)").bitcast(I32))
-        nc.sync.dma_start(w_raw[1][:], w_rows[:, :, HALF:])
+        w_raw = [sb.tile([P, PACK, PACK * groups], F32, name="w_raw%d" % first) for first, groups, on_vector in W_PIECES]
+
+        def load_w(i):
+            first, groups = W_PIECES[i][:2]
+            nc.sync.dma_start(w_raw[i][:], w_rows[:, :, PACK * first : PACK * (first + groups)])
+
+        load_w(0)
+        for q in range(QUADRANTS):
+            nc.sync.dma_start(x_scale_rows[32 * q : 32 * q + 4, :].bitcast(I32), x_scales[0, 4 * q : 4 * q + 4, :].bitcast(I32))
+        offs_t = load_list("offs_t", offs)
+        x_word_rows = sb.tile([P, T], U32, name="x_word_rows", align_bytes=64)
+        nc.sync.dma_start(x_word_rows[:].bitcast(I32), x_words[0].rearrange("p n t -> p (n t)").bitcast(I32))
+        load_w(1)
+        load_w(2)
         ga_t = sb.tile([P, PACK], F32, name="ga_t")
         gb_t = sb.tile([P, PACK], F32, name="gb_t")
         nc.sync.dma_start(gb_t[:], gb.rearrange("(p t) o -> p (t o)", t=PACK))
         nc.sync.dma_start(ga_t[:], ga.rearrange("(p t) o -> p (t o)", t=PACK))
-        n4_t = list_tile("n4_t", n4)
-        n3_t = list_tile("n3_t", n3)
-        n1_t = list_tile("n1_t", n1)
-        n5_t = list_tile("n5_t", n5)
-        n2_t = list_tile("n2_t", n2)
-        n6_t = list_tile("n6_t", n6)
+        n4_t = load_list("n4_t", n4)
+        n3_t = load_list("n3_t", n3)
+        n1_t = load_list("n1_t", n1)
+        n5_t = load_list("n5_t", n5)
+        n2_t = load_list("n2_t", n2)
+        n6_t = load_list("n6_t", n6)
 
         one = sb.tile([P, 1], F32, name="one")
         nc.vector.memset(one[:], 1.0)
@@ -62,40 +77,40 @@ def tile_picked_selfhopnfolddsend_none_p_kernel(tc, x_words, x_scales, w1, ga, g
         nc.vector.memset(ident[:], 0.0)
         make_identity(nc, ident[:], nomemset=True)
 
-        xgs = sb.tile([P, S], U8, name="xgs", align_bytes=64)
-        nc.vector.tensor_copy(xgs[:], xs[:].indirect(offs_t[:]))
-        xgw = sb.tile([P, S], U32, name="xgw", tag="xs", align_bytes=64)
-        nc.vector.tensor_copy(xgw[:], xw[:].indirect(offs_t[:]))
+        x_scale = sb.tile([P, S], U8, name="x_scale", align_bytes=64)
+        nc.vector.tensor_copy(x_scale[:], x_scale_rows[:].indirect(offs_t[:]))
+        x_code = sb.tile([P, S], U32, name="x_code", tag="x_scale_rows", align_bytes=64)
+        nc.vector.tensor_copy(x_code[:], x_word_rows[:].indirect(offs_t[:]))
 
-        safe = sb.tile([P, PACK], F32, name="safe")
-        nc.vector.scalar_tensor_tensor(safe[:], ga_t[:], 0.0, ga_t[:], ALU.is_equal, ALU.add)
-        inv = sb.tile([P, PACK], F32, name="inv")
-        nc.vector.reciprocal(inv[:], safe[:])
+        ga_or_one = sb.tile([P, PACK], F32, name="ga_or_one")
+        nc.vector.scalar_tensor_tensor(ga_or_one[:], ga_t[:], 0.0, ga_t[:], ALU.is_equal, ALU.add)
+        ga_inverse = sb.tile([P, PACK], F32, name="ga_inverse")
+        nc.vector.reciprocal(ga_inverse[:], ga_or_one[:])
 
         w_bf = sb.tile([P, PACK, P, PACK], BF16, name="w_bf", align_bytes=64)
-        M2 = P // 2
-        for h in range(2):
-            for copy, lo, hi in ((nc.vector.tensor_copy, 0, 40), (nc.scalar.copy, 40, M2)):
-                copy(
-                    w_bf[:, :, h * M2 + lo : h * M2 + hi, :].rearrange("p t m j -> p m j t"),
-                    w_raw[h][:].rearrange("p j (m t) -> p m j t", t=PACK)[:, lo:hi],
-                )
-        wq = sb.tile([P, S], U32, name="wq", align_bytes=64)
-        wsc = sb.tile([P, S], U8, name="wsc", align_bytes=64)
-        y_ps = []
+        for raw, (first, groups, on_vector) in zip(w_raw, W_PIECES):
+            for copy, lo, hi in ((nc.vector.tensor_copy, 0, on_vector), (nc.scalar.copy, on_vector, groups)):
+                if hi > lo:
+                    copy(
+                        w_bf[:, :, first + lo : first + hi, :].rearrange("p t m j -> p m j t"),
+                        raw[:].rearrange("p j (m t) -> p m j t", t=PACK)[:, lo:hi],
+                    )
+        w_code = sb.tile([P, S], U32, name="w_code", align_bytes=64)
+        w_scale = sb.tile([P, S], U8, name="w_scale", align_bytes=64)
+        y_pieces = []
         for t in range(PACK):
-            cols = slice(t * P, (t + 1) * P)
-            nc.vector.quantize_mx(out=wq[:, cols].bitcast(FP8X4), scales=wsc[:, cols], in_=w_bf[:, t].rearrange("p m j -> p (m j)"))
+            plane = slice(t * P, (t + 1) * P)
+            nc.vector.quantize_mx(out=w_code[:, plane].bitcast(FP8X4), scales=w_scale[:, plane], in_=w_bf[:, t].rearrange("p m j -> p (m j)"))
             pieces = []
             for lo, hi, tag in ((0, HALF, "y0"), (HALF, S, "s0")) if t == 0 else ((0, S, "y%d" % t),):
                 bank = psum.tile([P, S], F32, name="y%d_%d" % (t, lo), tag=tag)
-                nc.tensor.matmul_mx(out=bank[:, lo:hi], lhsT=wq[:, cols].bitcast(FP8X4), lhsT_scale=wsc[:, cols],
-                                    rhs=xgw[:, lo:hi].bitcast(FP8X4), rhs_scale=xgs[:, lo:hi], start=True, stop=True)
+                nc.tensor.matmul_mx(out=bank[:, lo:hi], lhsT=w_code[:, plane].bitcast(FP8X4), lhsT_scale=w_scale[:, plane],
+                                    rhs=x_code[:, lo:hi].bitcast(FP8X4), rhs_scale=x_scale[:, lo:hi], start=True, stop=True)
                 pieces.append((slice(lo, hi), bank))
-            y_ps.append(pieces)
+            y_pieces.append(pieces)
 
         def scaled_y(dst, t, gain):
-            for cols, bank in y_ps[t]:
+            for cols, bank in y_pieces[t]:
                 nc.scalar.activation(dst[:, cols], bank[:, cols], ACT.Copy, scale=gain[:, t : t + 1])
 
         ds = [sb.tile([P, S + spare * HALF], F32, name="ds%d" % t) for t, spare in enumerate((2, 1, 0, 0))]
@@ -106,143 +121,136 @@ def tile_picked_selfhopnfolddsend_none_p_kernel(tc, x_words, x_scales, w1, ga, g
             nc.vector.tensor_scalar(pb[t], ds[t][:].indirect(n4_t[:]), -0.5, 0.0, ALU.mult, ALU.add)
             nc.vector.tensor_copy(pa[t], ds[t][:].indirect(n3_t[:]))
 
-        def put_pairs(t):
-            nc.vector.tensor_tensor(ds[t][:].indirect(n4_t[:]), pa[t], pb[t], ALU.add)
-
-        (cols_a, bank_a), (cols_b, bank_b) = y_ps[0]
+        (cols_a, bank_a), (cols_b, bank_b) = y_pieces[0]
         nc.scalar.activation(ds[0][:, cols_a], bank_a[:, cols_a], ACT.Copy, scale=gb_t[:, 0:1])
         nc.vector.tensor_scalar(ds[0][:, cols_b], bank_b[:, cols_b], gb_t[:, 0:1], None, ALU.mult)
         fetch_pairs(0)
 
-        gst = sb.tile([P, PACK, S], F32, name="gst")
+        neg_st = sb.tile([P, PACK, S], F32, name="neg_st")
         for t in range(PACK):
-            ya = sb.tile([P, 2 * S], F32, name="ya%d" % t)
-            ya2 = sb.tile([P, S], F32, name="ya2%d" % t)
-            scaled_y(ya, t, ga_t)
-            scaled_y(ya2, t, ga_t)
-            nc.vector.tensor_tensor(gst[:, t, :], ya[:].indirect(n1_t[:]), ya2[:], ALU.subtract)
+            y_window = sb.tile([P, WIDE], F32, name="y_window%d" % t)
+            y_plain = sb.tile([P, S], F32, name="y_plain%d" % t)
+            scaled_y(y_window, t, ga_t)
+            scaled_y(y_plain, t, ga_t)
+            nc.vector.tensor_tensor(neg_st[:, t, :], y_window[:].indirect(n1_t[:]), y_plain[:], ALU.subtract)
 
         for t in range(1, PACK):
             scaled_y(ds[t], t, gb_t)
             fetch_pairs(t)
         for t in range(PACK):
-            put_pairs(t)
+            nc.vector.tensor_tensor(ds[t][:].indirect(n4_t[:]), pa[t], pb[t], ALU.add)
 
-        logs = []
+        log_size = [sb.tile([P, WIDE], F32, name="log_size%d" % t) for t in range(PACK)]
         for t in range(PACK):
-            lg = sb.tile([P, 2 * S], F32, name="lg%d" % t)
-            nc.scalar.activation(lg[:, S:], gst[:, t, :], ACT.Abs, scale=inv[:, t : t + 1])
-            logs.append(lg)
+            nc.scalar.activation(log_size[t][:, S:], neg_st[:, t, :], ACT.Abs, scale=ga_inverse[:, t : t + 1])
         for t in range(PACK):
-            nc.scalar.activation(logs[t][:, :S], logs[t][:, S:], ACT.Ln, bias=0.5)
+            nc.scalar.activation(log_size[t][:, :S], log_size[t][:, S:], ACT.Ln, bias=0.5)
 
-        rg = sb.tile([P, PACK, S], F32, name="rg")
-        z2 = sb.tile([P, PACK, S], F32, name="z2")
-        half_ds = []
+        inverse_size = sb.tile([P, PACK, S], F32, name="inverse_size")
+        neg_z2 = sb.tile([P, PACK, S], F32, name="neg_z2")
+        half_ds = [sb.tile([P, WIDE], F32, name="half_ds%d" % t) for t in range(PACK)]
 
-        def halve(t):
-            hd = sb.tile([P, 2 * S], F32, name="hd%d" % t)
-            nc.scalar.activation(hd[:, :S], ds[t][:, :S], ACT.Copy, scale=0.5)
-            half_ds.append(hd)
+        def fetch_inverse_size(t):
+            nc.scalar.activation(inverse_size[:, t, :], log_size[t][:].indirect(n2_t[:]), ACT.Exp, scale=-1.0)
 
-        def recip(t):
-            nc.scalar.activation(rg[:, t, :], logs[t][:].indirect(n2_t[:]), ACT.Exp, scale=-1.0)
+        def halve_ds(t):
+            nc.scalar.activation(half_ds[t][:, :S], ds[t][:, :S], ACT.Copy, scale=0.5)
 
-        recip(0)
-        halve(0)
-        halve(1)
-        recip(1)
-        halve(2)
-        halve(3)
-        recip(2)
-        recip(3)
+        for t in range(2):
+            fetch_inverse_size(t)
+            halve_ds(2 * t)
+            halve_ds(2 * t + 1)
+        for t in range(2, PACK):
+            fetch_inverse_size(t)
+
         for t in range(PACK):
             for lo, hi in ((0, S),) if t < PACK - 1 else ((0, HALF), (HALF, S)):
-                nc.vector.tensor_tensor(z2[:, t, lo:hi], half_ds[t][:].indirect(n5_t[:, lo // 16 : hi // 16]), ds[t][:, lo:hi], ALU.subtract)
+                nc.vector.tensor_tensor(neg_z2[:, t, lo:hi], half_ds[t][:].indirect(entries(n5_t, lo, hi)), ds[t][:, lo:hi], ALU.subtract)
 
-        zq = sb.tile([P, S], U32, name="zq", align_bytes=64)
-        zs = sb.tile([P, S], U8, name="zs", align_bytes=64)
-        z2q = sb.tile([P, S], U32, name="z2q", align_bytes=64)
-        z2s = sb.tile([P, S], U8, name="z2s", align_bytes=64)
+        z_code = sb.tile([P, S], U32, name="z_code", align_bytes=64)
+        z_scale = sb.tile([P, S], U8, name="z_scale", align_bytes=64)
+        z2_code = sb.tile([P, S], U32, name="z2_code", align_bytes=64)
+        z2_scale = sb.tile([P, S], U8, name="z2_scale", align_bytes=64)
 
-        def product(h):
-            us = slice(2 * h, 2 * h + 2)
+        def multiply_z(h):
+            planes = slice(2 * h, 2 * h + 2)
             z_bf = sb.tile([P, 2, P, PACK], BF16, name="z_bf%d" % h, align_bytes=64)
             nc.vector.tensor_tensor(
                 z_bf[:].rearrange("p u m t -> p m t u"),
-                gst[:].rearrange("p t (m u) -> p m t u", u=PACK)[:, :, :, us],
-                rg[:].rearrange("p t (m u) -> p m t u", u=PACK)[:, :, :, us],
+                neg_st[:].rearrange("p t (m u) -> p m t u", u=PACK)[:, :, :, planes],
+                inverse_size[:].rearrange("p t (m u) -> p m t u", u=PACK)[:, :, :, planes],
                 ALU.mult,
             )
             return z_bf
 
         def quantise_z(h, z_bf):
             cols = slice(h * HALF, (h + 1) * HALF)
-            nc.vector.quantize_mx(out=zq[:, cols].bitcast(FP8X4), scales=zs[:, cols], in_=z_bf[:].rearrange("p u m t -> p (u m t)"))
+            nc.vector.quantize_mx(out=z_code[:, cols].bitcast(FP8X4), scales=z_scale[:, cols], in_=z_bf[:].rearrange("p u m t -> p (u m t)"))
 
-        def weave(lo, hi):
+        def quantise_z2(lo, hi):
             z2_bf = sb.tile([P, hi - lo, PACK], BF16, name="z2_bf%d" % lo, align_bytes=64)
             nc.scalar.copy(
-                z2_bf[:].rearrange("p (c i) t -> p c t i", i=4),
-                z2[:, :, lo:hi].rearrange("p t (c i) -> p c t i", i=4),
+                z2_bf[:].rearrange("p (c i) t -> p c t i", i=LINE),
+                neg_z2[:, :, lo:hi].rearrange("p t (c i) -> p c t i", i=LINE),
             )
-            nc.vector.quantize_mx(out=z2q[:, lo:hi].bitcast(FP8X4), scales=z2s[:, lo:hi], in_=z2_bf[:].rearrange("p j t -> p (j t)"))
+            nc.vector.quantize_mx(out=z2_code[:, lo:hi].bitcast(FP8X4), scales=z2_scale[:, lo:hi], in_=z2_bf[:].rearrange("p j t -> p (j t)"))
 
-        first = product(0)
-        weave(0, P)
-        quantise_z(0, first)
-        second = product(1)
-        weave(P, HALF)
-        weave(HALF, S)
-        quantise_z(1, second)
+        z_first = multiply_z(0)
+        quantise_z2(0, P)
+        quantise_z(0, z_first)
+        z_second = multiply_z(1)
+        quantise_z2(P, HALF)
+        quantise_z2(HALF, S)
+        quantise_z(1, z_second)
 
-        s_ps = [psum.tile([P, S], F32, name="s%d" % u, tag="s%d" % u) for u in range(PACK)]
+        s_bank = [psum.tile([P, S], F32, name="s%d" % u, tag="s%d" % u) for u in range(PACK)]
         rl = [sb.tile([P, S], F32, name="rl%d" % u) for u in range(PACK)]
-        hs = [sb.tile([P, S], F32, name="hs%d" % u) for u in range(PACK - 1)]
-        ds2 = [sb.tile([P, 2 * S], F32, name="ds2%d" % u) for u in range(PACK)]
-        out_rows = out.rearrange("(m u) j -> u m j", u=PACK)
+        neg_half_s = [sb.tile([P, S], F32, name="neg_half_s%d" % u) for u in range(PACK - 1)]
+        ds2 = [sb.tile([P, WIDE], F32, name="ds2%d" % u) for u in range(PACK)]
+        out_planes = out.rearrange("(m u) j -> u m j", u=PACK)
 
         def send(u, *edges):
             lo, hi = edges[0], edges[-1]
             cols = slice(lo, hi)
-            rows = slice(u * P, (u + 1) * P)
-            bank = s_ps[u] if hi == S else psum.tile([P, S], F32, name="early%d" % u, tag="y%d" % (2 + u))
+            plane = slice(u * P, (u + 1) * P)
+            bank = s_bank[u] if hi == S else psum.tile([P, S], F32, name="early%d" % u, tag="y%d" % (2 + u))
             for a, b in zip(edges, edges[1:]):
-                nc.tensor.matmul_mx(out=bank[:, a:b], lhsT=zq[:, rows].bitcast(FP8X4), lhsT_scale=zs[:, rows],
-                                    rhs=z2q[:, a:b].bitcast(FP8X4), rhs_scale=z2s[:, a:b], start=True, stop=True)
+                nc.tensor.matmul_mx(out=bank[:, a:b], lhsT=z_code[:, plane].bitcast(FP8X4), lhsT_scale=z_scale[:, plane],
+                                    rhs=z2_code[:, a:b].bitcast(FP8X4), rhs_scale=z2_scale[:, a:b], start=True, stop=True)
             nc.scalar.activation(rl[u][:, cols], bank[:, cols], ACT.Relu, scale=0.0625)
-            nc.vector.tensor_copy(ds2[u][:].indirect(n6_t[:, lo // 16 : hi // 16]), rl[u][:, cols])
+            nc.vector.tensor_copy(ds2[u][:].indirect(entries(n6_t, lo, hi)), rl[u][:, cols])
             if u < PACK - 1:
-                nc.scalar.activation(hs[u][:, cols], bank[:, cols], ACT.Copy, scale=-0.03125)
+                nc.scalar.activation(neg_half_s[u][:, cols], bank[:, cols], ACT.Copy, scale=-0.03125)
 
-        def finish(u):
-            res = sb.tile([P, S], F32, name="res%d" % u)
-            if u == PACK - 1:
-                for h in range(2):
-                    cols = slice(h * HALF, (h + 1) * HALF)
-                    nc.vector.scalar_tensor_tensor(res[:, cols], s_ps[u][:, cols], -0.03125, ds2[u][:, cols], ALU.mult, ALU.add)
-                    nc.sync.dma_start(out_rows[u][:, cols], res[:, cols])
-            else:
-                turned = psum.tile([P, S], F32, name="turned%d" % u, tag="y%d" % (u % 2))
-                for k, term in enumerate((hs[u], ds2[u])):
-                    for b in range(PACK):
-                        blk = slice(b * P, (b + 1) * P)
-                        nc.tensor.matmul(turned[:, blk], term[:, blk], ident[:], is_transpose=True,
-                                         start=(k == 0 and b == 0), stop=(k == 1 and b == PACK - 1))
-                turned_sb = sb.tile([P, S], F32, name="turned_sb%d" % u)
-                nc.scalar.copy(turned_sb[:], turned[:])
-                back = psum.tile([P, S], F32, name="back%d" % u, tag="y%d" % (2 + u % 2))
+        def add_by_transposes(u):
+            result = sb.tile([P, S], F32, name="result%d" % u)
+            turned = psum.tile([P, S], F32, name="turned%d" % u, tag="y%d" % (u % 2))
+            for k, term in enumerate((neg_half_s[u], ds2[u])):
                 for b in range(PACK):
-                    blk = slice(b * P, (b + 1) * P)
-                    nc.tensor.transpose(back[:, blk], turned_sb[:, blk], ident[:])
-                nc.scalar.copy(res[:], back[:])
-                nc.scalar.dma_start(out_rows[u], res[:])
+                    block = slice(b * P, (b + 1) * P)
+                    nc.tensor.matmul(turned[:, block], term[:, block], ident[:], is_transpose=True,
+                                     start=(k == 0 and b == 0), stop=(k == 1 and b == PACK - 1))
+            turned_sb = sb.tile([P, S], F32, name="turned_sb%d" % u)
+            nc.scalar.copy(turned_sb[:], turned[:])
+            back = psum.tile([P, S], F32, name="back%d" % u, tag="y%d" % (2 + u % 2))
+            for b in range(PACK):
+                block = slice(b * P, (b + 1) * P)
+                nc.tensor.transpose(back[:, block], turned_sb[:, block], ident[:])
+            nc.scalar.copy(result[:], back[:])
+            nc.scalar.dma_start(out_planes[u], result[:])
 
-        send(0, 0, P)
-        send(1, 0, P)
-        send(0, P, HALF, S)
-        send(1, P, HALF, S)
-        send(2, 0, S)
-        send(3, 0, S)
-        for u in range(PACK):
-            finish(u)
+        def add_on_vector(u):
+            result = sb.tile([P, S], F32, name="result%d" % u)
+            for cols in (slice(0, S - LAST_STORE), slice(S - LAST_STORE, S)):
+                nc.vector.scalar_tensor_tensor(result[:, cols], s_bank[u][:, cols], -0.03125, ds2[u][:, cols], ALU.mult, ALU.add)
+                nc.sync.dma_start(out_planes[u][:, cols], result[:, cols])
+
+        for u in range(2):
+            send(u, 0, P)
+        for u in range(2):
+            send(u, P, HALF, S)
+        for u in range(2, PACK):
+            send(u, 0, S)
+        for u in range(PACK - 1):
+            add_by_transposes(u)
+        add_on_vector(PACK - 1)

from contextlib import ExitStack

import concourse.mybir as mybir
from concourse.masks import make_identity

F32 = mybir.dt.float32
BF16 = mybir.dt.bfloat16
I32 = mybir.dt.int32
U32 = mybir.dt.uint32
U16 = mybir.dt.uint16
U8 = mybir.dt.uint8
FP8X4 = mybir.dt.float8_e4m3fn_x4
ACT = mybir.ActivationFunctionType
ALU = mybir.AluOpType

P = 128
PACK = 4
QUADRANTS = 4
STRIPE = 16
LINE = 4
T = 2048
S = 512
HALF = S // 2
WIDE = 2 * S
W_PIECES = ((0, 64, 40), (64, 32, 0), (96, 32, 20))
LAST_STORE = 128
FLOPS = 2 * 2 * S * S * S


def tile_picked_selfhopnfolddsend_none_p_kernel(tc, x_words, x_scales, w1, ga, gb, offs, n1, n2, n3, n4, n5, n6, out):
    nc = tc.nc
    with ExitStack() as ctx:
        sb = ctx.enter_context(tc.tile_pool(name="sb", bufs=1))
        psum = ctx.enter_context(tc.psum_pool(name="psum", bufs=1))

        def load_list(name, src):
            tile = sb.tile([P, src.shape[1]], U16, name=name)
            nc.sync.dma_start(tile[:], src)
            return tile

        def entries(list_tile, lo, hi):
            return list_tile[:, lo // STRIPE : hi // STRIPE]

        x_scale_rows = sb.tile([P, T], U8, name="x_scale_rows", tag="x_scale_rows", align_bytes=64)
        nc.vector.memset(x_scale_rows[:].bitcast(I32), 0)
        w_rows = w1.rearrange("(p j) c -> p j c", j=PACK)
        w_raw = [sb.tile([P, PACK, PACK * groups], F32, name="w_raw%d" % first) for first, groups, on_vector in W_PIECES]

        def load_w(i):
            first, groups = W_PIECES[i][:2]
            nc.sync.dma_start(w_raw[i][:], w_rows[:, :, PACK * first : PACK * (first + groups)])

        load_w(0)
        for q in range(QUADRANTS):
            nc.sync.dma_start(x_scale_rows[32 * q : 32 * q + 4, :].bitcast(I32), x_scales[0, 4 * q : 4 * q + 4, :].bitcast(I32))
        offs_t = load_list("offs_t", offs)
        x_word_rows = sb.tile([P, T], U32, name="x_word_rows", align_bytes=64)
        nc.sync.dma_start(x_word_rows[:].bitcast(I32), x_words[0].rearrange("p n t -> p (n t)").bitcast(I32))
        load_w(1)
        load_w(2)
        ga_t = sb.tile([P, PACK], F32, name="ga_t")
        gb_t = sb.tile([P, PACK], F32, name="gb_t")
        nc.sync.dma_start(gb_t[:], gb.rearrange("(p t) o -> p (t o)", t=PACK))
        nc.sync.dma_start(ga_t[:], ga.rearrange("(p t) o -> p (t o)", t=PACK))
        n4_t = load_list("n4_t", n4)
        n3_t = load_list("n3_t", n3)
        n1_t = load_list("n1_t", n1)
        n5_t = load_list("n5_t", n5)
        n2_t = load_list("n2_t", n2)
        n6_t = load_list("n6_t", n6)

        one = sb.tile([P, 1], F32, name="one")
        nc.vector.memset(one[:], 1.0)
        warm = sb.tile([P, 1], F32, name="warm")
        nc.scalar.activation(warm[:], one[:], ACT.Ln)
        ident = sb.tile([P, P], F32, name="ident")
        nc.vector.memset(ident[:], 0.0)
        make_identity(nc, ident[:], nomemset=True)

        x_scale = sb.tile([P, S], U8, name="x_scale", align_bytes=64)
        nc.vector.tensor_copy(x_scale[:], x_scale_rows[:].indirect(offs_t[:]))
        x_code = sb.tile([P, S], U32, name="x_code", tag="x_scale_rows", align_bytes=64)
        nc.vector.tensor_copy(x_code[:], x_word_rows[:].indirect(offs_t[:]))

        ga_or_one = sb.tile([P, PACK], F32, name="ga_or_one")
        nc.vector.scalar_tensor_tensor(ga_or_one[:], ga_t[:], 0.0, ga_t[:], ALU.is_equal, ALU.add)
        ga_inverse = sb.tile([P, PACK], F32, name="ga_inverse")
        nc.vector.reciprocal(ga_inverse[:], ga_or_one[:])

        w_bf = sb.tile([P, PACK, P, PACK], BF16, name="w_bf", align_bytes=64)
        for raw, (first, groups, on_vector) in zip(w_raw, W_PIECES):
            for copy, lo, hi in ((nc.vector.tensor_copy, 0, on_vector), (nc.scalar.copy, on_vector, groups)):
                if hi > lo:
                    copy(
                        w_bf[:, :, first + lo : first + hi, :].rearrange("p t m j -> p m j t"),
                        raw[:].rearrange("p j (m t) -> p m j t", t=PACK)[:, lo:hi],
                    )
        w_code = sb.tile([P, S], U32, name="w_code", align_bytes=64)
        w_scale = sb.tile([P, S], U8, name="w_scale", align_bytes=64)
        y_pieces = []
        for t in range(PACK):
            plane = slice(t * P, (t + 1) * P)
            nc.vector.quantize_mx(out=w_code[:, plane].bitcast(FP8X4), scales=w_scale[:, plane], in_=w_bf[:, t].rearrange("p m j -> p (m j)"))
            pieces = []
            for lo, hi, tag in ((0, HALF, "y0"), (HALF, S, "s0")) if t == 0 else ((0, S, "y%d" % t),):
                bank = psum.tile([P, S], F32, name="y%d_%d" % (t, lo), tag=tag)
                nc.tensor.matmul_mx(out=bank[:, lo:hi], lhsT=w_code[:, plane].bitcast(FP8X4), lhsT_scale=w_scale[:, plane],
                                    rhs=x_code[:, lo:hi].bitcast(FP8X4), rhs_scale=x_scale[:, lo:hi], start=True, stop=True)
                pieces.append((slice(lo, hi), bank))
            y_pieces.append(pieces)

        def scaled_y(dst, t, gain):
            for cols, bank in y_pieces[t]:
                nc.scalar.activation(dst[:, cols], bank[:, cols], ACT.Copy, scale=gain[:, t : t + 1])

        ds = [sb.tile([P, S + spare * HALF], F32, name="ds%d" % t) for t, spare in enumerate((2, 1, 0, 0))]
        pa = [sb.tile([P, HALF], F32, name="pa%d" % t)[:] for t in range(3)] + [ds[1][:, S:]]
        pb = [sb.tile([P, HALF], F32, name="pb%d" % t)[:] for t in range(2)] + [ds[0][:, S : S + HALF], ds[0][:, S + HALF :]]

        def fetch_pairs(t):
            nc.vector.tensor_scalar(pb[t], ds[t][:].indirect(n4_t[:]), -0.5, 0.0, ALU.mult, ALU.add)
            nc.vector.tensor_copy(pa[t], ds[t][:].indirect(n3_t[:]))

        (cols_a, bank_a), (cols_b, bank_b) = y_pieces[0]
        nc.scalar.activation(ds[0][:, cols_a], bank_a[:, cols_a], ACT.Copy, scale=gb_t[:, 0:1])
        nc.vector.tensor_scalar(ds[0][:, cols_b], bank_b[:, cols_b], gb_t[:, 0:1], None, ALU.mult)
        fetch_pairs(0)

        neg_st = sb.tile([P, PACK, S], F32, name="neg_st")
        for t in range(PACK):
            y_window = sb.tile([P, WIDE], F32, name="y_window%d" % t)
            y_plain = sb.tile([P, S], F32, name="y_plain%d" % t)
            scaled_y(y_window, t, ga_t)
            scaled_y(y_plain, t, ga_t)
            nc.vector.tensor_tensor(neg_st[:, t, :], y_window[:].indirect(n1_t[:]), y_plain[:], ALU.subtract)

        for t in range(1, PACK):
            scaled_y(ds[t], t, gb_t)
            fetch_pairs(t)
        for t in range(PACK):
            nc.vector.tensor_tensor(ds[t][:].indirect(n4_t[:]), pa[t], pb[t], ALU.add)

        log_size = [sb.tile([P, WIDE], F32, name="log_size%d" % t) for t in range(PACK)]
        for t in range(PACK):
            nc.scalar.activation(log_size[t][:, S:], neg_st[:, t, :], ACT.Abs, scale=ga_inverse[:, t : t + 1])
        for t in range(PACK):
            nc.scalar.activation(log_size[t][:, :S], log_size[t][:, S:], ACT.Ln, bias=0.5)

        inverse_size = sb.tile([P, PACK, S], F32, name="inverse_size")
        neg_z2 = sb.tile([P, PACK, S], F32, name="neg_z2")
        half_ds = [sb.tile([P, WIDE], F32, name="half_ds%d" % t) for t in range(PACK)]

        def fetch_inverse_size(t):
            nc.scalar.activation(inverse_size[:, t, :], log_size[t][:].indirect(n2_t[:]), ACT.Exp, scale=-1.0)

        def halve_ds(t):
            nc.scalar.activation(half_ds[t][:, :S], ds[t][:, :S], ACT.Copy, scale=0.5)

        for t in range(2):
            fetch_inverse_size(t)
            halve_ds(2 * t)
            halve_ds(2 * t + 1)
        for t in range(2, PACK):
            fetch_inverse_size(t)

        for t in range(PACK):
            for lo, hi in ((0, S),) if t < PACK - 1 else ((0, HALF), (HALF, S)):
                nc.vector.tensor_tensor(neg_z2[:, t, lo:hi], half_ds[t][:].indirect(entries(n5_t, lo, hi)), ds[t][:, lo:hi], ALU.subtract)

        z_code = sb.tile([P, S], U32, name="z_code", align_bytes=64)
        z_scale = sb.tile([P, S], U8, name="z_scale", align_bytes=64)
        z2_code = sb.tile([P, S], U32, name="z2_code", align_bytes=64)
        z2_scale = sb.tile([P, S], U8, name="z2_scale", align_bytes=64)

        def multiply_z(h):
            planes = slice(2 * h, 2 * h + 2)
            z_bf = sb.tile([P, 2, P, PACK], BF16, name="z_bf%d" % h, align_bytes=64)
            nc.vector.tensor_tensor(
                z_bf[:].rearrange("p u m t -> p m t u"),
                neg_st[:].rearrange("p t (m u) -> p m t u", u=PACK)[:, :, :, planes],
                inverse_size[:].rearrange("p t (m u) -> p m t u", u=PACK)[:, :, :, planes],
                ALU.mult,
            )
            return z_bf

        def quantise_z(h, z_bf):
            cols = slice(h * HALF, (h + 1) * HALF)
            nc.vector.quantize_mx(out=z_code[:, cols].bitcast(FP8X4), scales=z_scale[:, cols], in_=z_bf[:].rearrange("p u m t -> p (u m t)"))

        def quantise_z2(lo, hi):
            z2_bf = sb.tile([P, hi - lo, PACK], BF16, name="z2_bf%d" % lo, align_bytes=64)
            nc.scalar.copy(
                z2_bf[:].rearrange("p (c i) t -> p c t i", i=LINE),
                neg_z2[:, :, lo:hi].rearrange("p t (c i) -> p c t i", i=LINE),
            )
            nc.vector.quantize_mx(out=z2_code[:, lo:hi].bitcast(FP8X4), scales=z2_scale[:, lo:hi], in_=z2_bf[:].rearrange("p j t -> p (j t)"))

        z_first = multiply_z(0)
        quantise_z2(0, P)
        quantise_z(0, z_first)
        z_second = multiply_z(1)
        quantise_z2(P, HALF)
        quantise_z2(HALF, S)
        quantise_z(1, z_second)

        s_bank = [psum.tile([P, S], F32, name="s%d" % u, tag="s%d" % u) for u in range(PACK)]
        rl = [sb.tile([P, S], F32, name="rl%d" % u) for u in range(PACK)]
        neg_half_s = [sb.tile([P, S], F32, name="neg_half_s%d" % u) for u in range(PACK - 1)]
        ds2 = [sb.tile([P, WIDE], F32, name="ds2%d" % u) for u in range(PACK)]
        out_planes = out.rearrange("(m u) j -> u m j", u=PACK)

        def send(u, *edges):
            lo, hi = edges[0], edges[-1]
            cols = slice(lo, hi)
            plane = slice(u * P, (u + 1) * P)
            bank = s_bank[u] if hi == S else psum.tile([P, S], F32, name="early%d" % u, tag="y%d" % (2 + u))
            for a, b in zip(edges, edges[1:]):
                nc.tensor.matmul_mx(out=bank[:, a:b], lhsT=z_code[:, plane].bitcast(FP8X4), lhsT_scale=z_scale[:, plane],
                                    rhs=z2_code[:, a:b].bitcast(FP8X4), rhs_scale=z2_scale[:, a:b], start=True, stop=True)
            nc.scalar.activation(rl[u][:, cols], bank[:, cols], ACT.Relu, scale=0.0625)
            nc.vector.tensor_copy(ds2[u][:].indirect(entries(n6_t, lo, hi)), rl[u][:, cols])
            if u < PACK - 1:
                nc.scalar.activation(neg_half_s[u][:, cols], bank[:, cols], ACT.Copy, scale=-0.03125)

        def add_by_transposes(u):
            result = sb.tile([P, S], F32, name="result%d" % u)
            turned = psum.tile([P, S], F32, name="turned%d" % u, tag="y%d" % (u % 2))
            for k, term in enumerate((neg_half_s[u], ds2[u])):
                for b in range(PACK):
                    block = slice(b * P, (b + 1) * P)
                    nc.tensor.matmul(turned[:, block], term[:, block], ident[:], is_transpose=True,
                                     start=(k == 0 and b == 0), stop=(k == 1 and b == PACK - 1))
            turned_sb = sb.tile([P, S], F32, name="turned_sb%d" % u)
            nc.scalar.copy(turned_sb[:], turned[:])
            back = psum.tile([P, S], F32, name="back%d" % u, tag="y%d" % (2 + u % 2))
            for b in range(PACK):
                block = slice(b * P, (b + 1) * P)
                nc.tensor.transpose(back[:, block], turned_sb[:, block], ident[:])
            nc.scalar.copy(result[:], back[:])
            nc.scalar.dma_start(out_planes[u], result[:])

        def add_on_vector(u):
            result = sb.tile([P, S], F32, name="result%d" % u)
            for cols in (slice(0, S - LAST_STORE), slice(S - LAST_STORE, S)):
                nc.vector.scalar_tensor_tensor(result[:, cols], s_bank[u][:, cols], -0.03125, ds2[u][:, cols], ALU.mult, ALU.add)
                nc.sync.dma_start(out_planes[u][:, cols], result[:, cols])

        for u in range(2):
            send(u, 0, P)
        for u in range(2):
            send(u, P, HALF, S)
        for u in range(2, PACK):
            send(u, 0, S)
        for u in range(PACK - 1):
            add_by_transposes(u)
        add_on_vector(PACK - 1)
